import numpy as np
import ml_dtypes


def mxq(x, axis, fmt="e4m3"):
    dtype, down = {"e4m3": (ml_dtypes.float8_e4m3fn, 7), "e5m2": (ml_dtypes.float8_e5m2, 14)}[fmt]
    v = np.moveaxis(np.asarray(x, np.float32).astype(ml_dtypes.bfloat16).astype(np.float64), axis, -1)
    blocks = v.reshape(v.shape[:-1] + (-1, 32))
    amax = np.abs(blocks).max(-1, keepdims=True)
    byte = np.maximum(np.where(amax > 0, np.frexp(amax)[1] - 1 + 127, 0) - down, 1)
    scale = np.exp2(byte - 127.0)
    codes = (blocks / scale).astype(np.float32).astype(dtype).astype(np.float64)
    return np.moveaxis((codes * scale).reshape(v.shape), -1, axis)


WIDE = False


def mx_kscale(k):
    if not WIDE:
        return np.ones(k)
    levels = np.array([10, -10, 5, -5, 0])
    if k % 512:
        return np.exp2(np.random.permutation(np.resize(levels, k // 32))).repeat(32)
    a = np.empty((k // 512, 16))
    for p in range(k // 512):
        a[p, :8] = np.random.permutation(np.resize(levels, 8))
        for g in range(8):
            far = levels[np.abs(levels - a[p, g]) >= 10]
            a[p, g + 8] = far[np.random.randint(len(far))]
    return np.exp2(a.ravel()).repeat(32)


BF16 = ml_dtypes.bfloat16


def bf(x):
    return np.asarray(x, np.float32).astype(BF16)


def f64(x):
    return np.asarray(x).astype(np.float64)


E2M1 = np.array([0.0, 0.5, 1.0, 1.5, 2.0, 3.0, 4.0, 6.0, -0.0, -0.5, -1.0, -1.5, -2.0, -3.0, -4.0, -6.0])


def pack_weight(w, fmt):
    k, n = w.shape
    w = f64(bf(w)).reshape(k // 32, 32, n)
    amax = np.abs(w).max(1)
    if fmt == "e4m3":
        byte = np.frexp(amax)[1] - 1 + 127 - 7
    else:
        mant, ex = np.frexp(amax / 6.0)
        byte = np.where(mant > 0.5, ex, ex - 1) + 127
    byte = np.clip(np.where(amax > 0, byte, 1), 1, 254)
    scaled = (w * np.exp2(127.0 - byte)[:, None, :]).reshape(k, n).astype(np.float32)
    by_word = np.ascontiguousarray(scaled.reshape(k // 512, 128, 4, n).transpose(0, 1, 3, 2))
    if fmt == "e4m3":
        words = by_word.astype(ml_dtypes.float8_e4m3fn).view(np.uint8)
    else:
        c = by_word.astype(ml_dtypes.float4_e2m1fn).view(np.uint8) & 0xF
        words = c[..., 0::2] | (c[..., 1::2] << 4)
    return np.ascontiguousarray(words), np.ascontiguousarray(byte.astype(np.uint8).reshape(k // 512, 16, n))


def unpack_weight(words, scales, fmt):
    g, p, n, _ = words.shape
    if fmt == "e4m3":
        vals = np.ascontiguousarray(words).view(ml_dtypes.float8_e4m3fn).astype(np.float64)
    else:
        nib = np.empty((g, p, n, 4), np.uint8)
        nib[..., 0::2] = words & 0xF
        nib[..., 1::2] = words >> 4
        vals = E2M1[nib]
    vals = vals * np.repeat(np.exp2(scales.astype(np.float64) - 127.0), 8, axis=1)[..., None]
    return vals.transpose(0, 1, 3, 2).reshape(g * 512, n)
def pack4(w):
    words, scales = pack_weight(w, "e2m1")
    return words.reshape(words.shape[0], 128, -1), scales


def unpack4(words, scales):
    return unpack_weight(words.reshape(words.shape[0], 128, -1, 2), scales, "e2m1")


T, K, F1, F2, N, R = 1024, 1024, 1536, 1024, 512, 512


def draw0():
    s1, s2 = mx_kscale(K), mx_kscale(K)
    t1, t2 = mx_kscale(F1), mx_kscale(F2)
    u = mx_kscale(T)
    d1 = np.random.standard_normal((F1, N)) / np.sqrt(F1) / t1[:, None]
    d1_words, d1_scales = pack4(d1)
    return {"x1": bf(np.random.standard_normal((T, K)) * s1 * u[:, None]),
            "x2": bf(np.random.standard_normal((T, K)) * s2 * u[:, None]),
            "e1": bf(np.random.standard_normal((K, F1)) / np.sqrt(K) / s1[:, None] * t1),
            "e2": bf(np.random.standard_normal((K, F2)) / np.sqrt(K) / s2[:, None] * t2),
            "d1_words": d1_words,
            "d1_scales": d1_scales,
            "d2": bf(np.random.standard_normal((F2, N)) / np.sqrt(F2) / t2[:, None]),
            "labels": bf(np.random.standard_normal((T, R)) / np.sqrt(T) / u[:, None])}


def core(x1, x2, e1, e2, d1_words, d1_scales, d2, labels):
    a1 = np.maximum(mxq(f64(x1), 1, "e4m3") @ mxq(f64(e1), 0, "e4m3"), 0.0)
    a2 = np.maximum(mxq(f64(x2), 1, "e4m3") @ mxq(f64(e2), 0, "e4m3"), 0.0)
    d1 = unpack4(d1_words, d1_scales)
    y = (mxq(a1, 1, "e4m3") @ d1) + (mxq(a2, 1, "e4m3") @ mxq(f64(d2), 0, "e4m3"))
    lab = mxq(f64(labels), 0, "e4m3")
    c1 = mxq(a1, 0, "e4m3").T @ lab
    c2 = mxq(a2, 0, "e4m3").T @ lab
    return y, c1, c2


def e4m3fn_bytes(y):
    return np.clip(np.asarray(y, np.float64), -448.0, 448.0).astype(np.float32).astype(ml_dtypes.float8_e4m3fn).view(np.uint8)


def e4m3fn_values(b):
    return np.asarray(b, np.uint8).view(ml_dtypes.float8_e4m3fn).astype(np.float64)


def setup_inputs():
    d = draw0()
    x0 = np.asarray(d['labels']).astype(np.float64)
    s = (np.max(np.abs(x0), axis=(1,), keepdims=True) / 448.0).astype(np.float32)
    out = {}
    for k, v in d.items():
        if k == 'labels':
            out['labels_bytes'] = e4m3fn_bytes(x0 / s.astype(np.float64))
            out['labels_scale'] = s
        else:
            out[k] = v
    return out


def reference(x1, x2, e1, e2, d1_words, d1_scales, d2, labels_bytes, labels_scale):
    return core(x1, x2, e1, e2, d1_words, d1_scales, d2, e4m3fn_values(labels_bytes) * labels_scale.astype(np.float64))

@@ -1,0 +1,346 @@
+from contextlib import ExitStack
+
+import concourse.mybir as mybir
+from concourse.masks import make_identity
+
+F32 = mybir.dt.float32
+BF16 = mybir.dt.bfloat16
+U32 = mybir.dt.uint32
+I32 = mybir.dt.int32
+U8 = mybir.dt.uint8
+E4M3 = mybir.dt.float8_e4m3fn
+E4M3X4 = mybir.dt.float8_e4m3fn_x4
+E2M1X4 = mybir.dt.float4_e2m1fn_x4
+ACT = mybir.ActivationFunctionType
+ALU = mybir.AluOpType
+
+T, K, F1, F2, N, R = 1024, 1024, 1536, 1024, 512, 512
+P = 128
+FLOPS = 2 * (T * K * (F1 + F2) + T * (F1 + F2) * (N + R))
+NG = 5
+NU = 2 * NG
+
+
+def tile_cross_layer_transcoder_s8_kernel(
+    tc, x1, x2, e1, e2, d1_words, d1_scales, d2, labels_bytes, labels_scale, out_0, out_1, out_2
+):
+    nc = tc.nc
+    with ExitStack() as ctx:
+        keep = ctx.enter_context(tc.tile_pool(name="keep", bufs=1))
+        pool = ctx.enter_context(tc.tile_pool(name="work", bufs=1))
+        psum = ctx.enter_context(tc.psum_pool(name="psum", bufs=1))
+        ctx.enter_context(tc.manual_schedule())
+
+        def tile(shape, dtype, tag, bufs):
+            return pool.tile(shape, dtype, name=tag, tag=tag, bufs=bufs, align_bytes=64)
+
+        def bank(tag, bufs):
+            return psum.tile([P, 512], F32, name=tag, tag=tag, bufs=bufs)
+
+        ident = keep.tile([P, P], F32, name="ident", align_bytes=64)
+        make_identity(nc, ident[:])
+        warm = keep.tile([P, 1], F32, name="warm", align_bytes=64)
+        nc.gpsimd.memset(warm[:], 0.0)
+        nc.scalar.activation(out=warm[:], in_=warm[:], func=ACT.Relu)
+        d1_sc = keep.tile([P, 3, 512], U8, name="d1_sc", align_bytes=64)
+        nc.gpsimd.memset(d1_sc[:].rearrange("p g n -> p (g n)").bitcast(I32), 0)
+
+        x_raw = {}
+        e_raw = {}
+        xs = [x1, x2]
+
+        def load_x(s, g, parts):
+            t = tile([P, 4, K], BF16, "x_raw", 3)
+            view = xs[s].rearrange("(g p j) k -> g p j k", p=P, j=4)[g]
+            step = 4 // parts
+            for i in range(parts):
+                nc.sync.dma_start(out=t[:, i * step : (i + 1) * step, :], in_=view[:, i * step : (i + 1) * step, :])
+            x_raw[s, g] = t
+
+        def load_e(g0, q, width, tag, bufs, e, col):
+            t = tile([P, 4, width], BF16, tag, bufs)
+            nc.sync.dma_start(
+                out=t[:], in_=e.rearrange("(q p j) c -> q p j c", p=P, j=4)[q][:, :, col : col + width]
+            )
+            for i in range(width // 512):
+                e_raw[g0 + i, q] = t[:, :, i * 512 : (i + 1) * 512]
+
+        t0 = tile([P, 4, K], BF16, "x_raw", 3)
+        x_raw[0, 0] = t0
+        v0 = x1.rearrange("(g p j) k -> g p j k", p=P, j=4)[0]
+        load_e(0, 0, 512, "e_a", 2, e1, 0)
+        nc.sync.dma_start(out=t0[:, 0:1, :], in_=v0[:, 0:1, :])
+        load_e(0, 1, 512, "e_a", 2, e1, 0)
+        for j in (1, 2, 3):
+            nc.sync.dma_start(out=t0[:, j : j + 1, :], in_=v0[:, j : j + 1, :])
+        load_x(0, 1, 2)
+        load_e(1, 0, 1024, "e_b", 4, e1, 512)
+        load_e(1, 1, 1024, "e_b", 4, e1, 512)
+        lab_sc = keep.tile([P, 2, 4], F32, name="lab_sc", align_bytes=64)
+        nc.sync.dma_start(out=lab_sc[:], in_=labels_scale.rearrange("(g p j) o -> p g (j o)", p=P, j=4))
+        lab_raw = keep.tile([P, 2, 4, R], U8, name="lab_raw", align_bytes=64)
+        nc.sync.dma_start(out=lab_raw[:], in_=labels_bytes.rearrange("(g p j) r -> p g j r", p=P, j=4))
+        load_x(1, 0, 1)
+        load_e(3, 0, 1024, "e_b", 4, e2, 0)
+        load_e(3, 1, 1024, "e_b", 4, e2, 0)
+        load_x(1, 1, 1)
+        d1_w = keep.tile([P, 3, 1024], U8, name="d1_w", align_bytes=64)
+        nc.sync.dma_start(out=d1_w[:], in_=d1_words.rearrange("g p c -> p g c"))
+        d1_si = d1_scales.bitcast(I32)
+        for quad in range(4):
+            nc.sync.dma_start(
+                out=d1_sc[32 * quad : 32 * quad + 4, :, :].rearrange("p g n -> p (g n)").bitcast(I32).rearrange(
+                    "p (g n) -> p g n", g=3
+                ),
+                in_=d1_si[:, 4 * quad : 4 * quad + 4, :].rearrange("g r n -> r g n"),
+            )
+        d2_raw = {}
+        for g in range(2):
+            t = tile([P, 4, N], BF16, "e_a", 2)
+            nc.sync.dma_start(out=t[:], in_=d2.rearrange("(g p j) n -> g p j n", p=P, j=4)[g])
+            d2_raw[g] = t
+
+        x_c, x_s, x_t = {}, {}, {}
+
+        def x_turn(s, g, j):
+            if j == 0:
+                x_c[s, g] = tile([P, 1024], U32, "x_c", 4)
+                x_s[s, g] = tile([P, 1024], U8, "x_s", 4)
+            tr = bank("tr", 2)
+            words = x_raw[s, g][:, j, :].bitcast(F32)
+            for q in range(2):
+                for u in range(2):
+                    i = 2 * q + u
+                    nc.tensor.transpose(
+                        tr[:, i * P : (i + 1) * P], words[:, 256 * q + u : 256 * (q + 1) : 2], ident[:]
+                    )
+            xt = tile([P, 1024], BF16, "x_t", 4)
+            nc.scalar.copy(
+                out=xt[:].bitcast(F32).rearrange("p (q t u) -> p q t u", q=2, u=2),
+                in_=tr[:].rearrange("p (q u t) -> p q t u", q=2, u=2),
+            )
+            x_t[s, g, j] = xt
+
+        def x_quant(s, g, j):
+            cols = slice(256 * j, 256 * (j + 1))
+            nc.vector.quantize_mx(
+                out=x_c[s, g][:, cols].bitcast(E4M3X4), scales=x_s[s, g][:, cols], in_=x_t[s, g, j][:]
+            )
+
+        def interleave(raw):
+            t = tile([P, 512, 4], BF16, "mix", 3)
+            nc.vector.tensor_copy(out=t[:], in_=raw.rearrange("p j c -> p c j"))
+            return t
+
+        def quant(codes, scales, src):
+            nc.vector.quantize_mx(out=codes.bitcast(E4M3X4), scales=scales, in_=src[:].rearrange("p c j -> p (c j)"))
+
+        e_c, e_s, e_m = {}, {}, {}
+
+        def e_mix(G, q):
+            if q == 0:
+                e_c[G] = tile([P, 2, 512], U32, "e_c", 4)
+                e_s[G] = tile([P, 2, 512], U8, "e_s", 4)
+            e_m[G, q] = interleave(e_raw[G, q])
+
+        def e_quant(G, q):
+            quant(e_c[G][:, q, :], e_s[G][:, q, :], e_m[G, q])
+
+        lab_c = keep.tile([P, 2, R], U32, name="lab_c", align_bytes=64)
+        lab_s = keep.tile([P, 2, R], U8, name="lab_s", align_bytes=64)
+        lab_b, lab_m = {}, {}
+
+        def lab_widen(g):
+            t = tile([P, 4, R], BF16, "lab_b", 1)
+            for j in range(4):
+                nc.vector.tensor_scalar(
+                    out=t[:, j, :],
+                    in0=lab_raw[:, g, j, :].bitcast(E4M3),
+                    scalar1=lab_sc[:, g, j : j + 1],
+                    scalar2=None,
+                    op0=ALU.mult,
+                )
+            lab_b[g] = t
+
+        def lab_mix(g):
+            lab_m[g] = interleave(lab_b[g][:])
+
+        def lab_quant(g):
+            quant(lab_c[:, g, :], lab_s[:, g, :], lab_m[g])
+
+        d2_c = keep.tile([P, 2, N], U32, name="d2_c", align_bytes=64)
+        d2_s = keep.tile([P, 2, N], U8, name="d2_s", align_bytes=64)
+        d2_m = {}
+
+        def d2_mix(g):
+            d2_m[g] = interleave(d2_raw[g][:])
+
+        def d2_quant(g):
+            quant(d2_c[:, g, :], d2_s[:, g, :], d2_m[g])
+
+        a_raw, a_m, a_t = {}, {}, {}
+        ac_c, ac_s, at_c, at_s = {}, {}, {}, {}
+
+        def stage1(n):
+            G, g = divmod(n, 2)
+            s = 0 if G < 3 else 1
+            a = tile([P, 4, 512], BF16, "a", 3)
+            a_raw[n] = a
+            for j in range(4):
+                acc = bank("s1", 3)
+                for q in range(2):
+                    cols = slice(256 * j + 128 * q, 256 * j + 128 * (q + 1))
+                    nc.tensor.matmul_mx(
+                        out=acc[:],
+                        lhsT=x_c[s, g][:, cols].bitcast(E4M3X4),
+                        lhsT_scale=x_s[s, g][:, cols],
+                        rhs=e_c[G][:, q, :].bitcast(E4M3X4),
+                        rhs_scale=e_s[G][:, q, :],
+                        start=(q == 0),
+                        stop=(q == 1),
+                    )
+                nc.scalar.activation(
+                    out=a[:, j, :].rearrange("p (u m e) -> p u m e", u=2, e=2),
+                    in_=acc[:].rearrange("p (m u e) -> p u m e", u=2, e=2),
+                    func=ACT.Relu,
+                )
+
+        def a_turn(n):
+            at = tile([P, 512, 4], BF16, "a_t", 2)
+            a_t[n] = at
+            words = a_raw[n][:].rearrange("p j f -> p (j f)").bitcast(F32)
+            out = at[:].rearrange("p t f -> p (t f)").bitcast(F32)
+            for h in range(2):
+                tr = bank("tr", 2)
+                for i in range(4):
+                    col = 512 * h + 128 * i
+                    nc.tensor.transpose(tr[:, i * P : (i + 1) * P], words[:, col : col + P], ident[:])
+                nc.scalar.copy(
+                    out=out[:, 512 * h : 512 * (h + 1)].rearrange("p (j t u) -> p j t u", j=2, u=2),
+                    in_=tr[:].rearrange("p (j u t) -> p j t u", j=2, u=2),
+                )
+
+        def a_mix(n):
+            t = tile([P, 512, 4], BF16, "a_m", 2)
+            src = a_raw[n][:].rearrange("p j (u m e) -> p u m e j", u=2, e=2)
+            dst = t[:].rearrange("p (m u e) j -> p u m e j", u=2, e=2)
+            for u in range(2):
+                nc.vector.tensor_copy(out=dst[:, u], in_=src[:, u])
+            a_m[n] = t
+
+        def ac_quant(n):
+            ac_c[n] = tile([P, 512], U32, "ac_c", 6)
+            ac_s[n] = tile([P, 512], U8, "ac_s", 6)
+            quant(ac_c[n][:], ac_s[n][:], a_m[n])
+
+        def at_quant(n):
+            at_c[n] = tile([P, 512], U32, "at_c", NU)
+            at_s[n] = tile([P, 512], U8, "at_s", NU)
+            quant(at_c[n][:], at_s[n][:], a_t[n])
+
+        outs = {}
+
+        def c_blocks(G, half, vec=False):
+            o = tile([P, 2, R], F32, "o", 4)
+            for i in range(2):
+                b = 2 * half + i
+                acc = bank("o", 3)
+                cols = slice(128 * b, 128 * (b + 1))
+                for g in range(2):
+                    n = 2 * G + g
+                    nc.tensor.matmul_mx(
+                        out=acc[:],
+                        lhsT=ac_c[n][:, cols].bitcast(E4M3X4),
+                        lhsT_scale=ac_s[n][:, cols],
+                        rhs=lab_c[:, g, :].bitcast(E4M3X4),
+                        rhs_scale=lab_s[:, g, :],
+                        start=(g == 0),
+                        stop=(g == 1),
+                    )
+                if vec and i == 1:
+                    nc.vector.tensor_copy(out=o[:, i, :], in_=acc[:])
+                else:
+                    nc.scalar.copy(out=o[:, i, :], in_=acc[:])
+            dst = out_1 if G < 3 else out_2
+            row = 512 * (G if G < 3 else G - 3) + 256 * half
+            nc.sync.dma_start(out=dst[row : row + 256, :].rearrange("(b p) r -> p b r", p=P), in_=o[:])
+
+        def y_blocks(g, half):
+            o = tile([P, 2, N], F32, "o", 4)
+            for i in range(2):
+                j = 2 * half + i
+                acc = bank("o", 3)
+                cols = slice(128 * j, 128 * (j + 1))
+                for G in range(NG):
+                    n = 2 * G + g
+                    if G < 3:
+                        rhs, rhs_scale = d1_w[:, G, :].bitcast(E2M1X4), d1_sc[:, G, :]
+                    else:
+                        rhs, rhs_scale = d2_c[:, G - 3, :].bitcast(E4M3X4), d2_s[:, G - 3, :]
+                    nc.tensor.matmul_mx(
+                        out=acc[:],
+                        lhsT=at_c[n][:, cols].bitcast(E4M3X4),
+                        lhsT_scale=at_s[n][:, cols],
+                        rhs=rhs,
+                        rhs_scale=rhs_scale,
+                        start=(G == 0),
+                        stop=(G == NG - 1),
+                    )
+                if i == 1:
+                    nc.vector.tensor_copy(out=o[:, i, :], in_=acc[:])
+                else:
+                    nc.scalar.copy(out=o[:, i, :], in_=acc[:])
+            dst = out_0.rearrange("(g p j) n -> g p j n", p=P, j=4)[g]
+            nc.sync.dma_start(out=dst[:, 2 * half : 2 * half + 2, :], in_=o[:])
+
+        for j in range(4):
+            x_turn(0, 0, j)
+        e_mix(0, 0)
+        e_mix(0, 1)
+        e_quant(0, 0)
+        x_quant(0, 0, 0)
+        e_quant(0, 1)
+        for j in range(1, 4):
+            x_quant(0, 0, j)
+
+        extra_x = {0: [(0, 1, 0), (0, 1, 1), (0, 1, 2), (0, 1, 3)]}
+        for i in range(4):
+            extra_x[1 + i] = [(1, i // 2, 2 * (i % 2)), (1, i // 2, 2 * (i % 2) + 1)]
+        for n in range(NU + 3):
+            if n < NU:
+                stage1(n)
+            for s, g, j in extra_x.get(n, []):
+                x_turn(s, g, j)
+            for s, g, j in extra_x.get(n, []):
+                x_quant(s, g, j)
+            if 1 <= n <= NU:
+                a_turn(n - 1)
+                a_mix(n - 1)
+            G, q = n // 2 + 1, n % 2
+            if G < NG:
+                e_mix(G, q)
+            if n == 0:
+                lab_widen(0)
+            if n == 1:
+                lab_widen(1)
+            if 2 <= n <= NU + 1:
+                at_quant(n - 2)
+            if G < NG:
+                e_quant(G, q)
+            if n in (0, 1):
+                lab_mix(n)
+            if n in (7, 8):
+                d2_mix(n - 7)
+            if 1 <= n <= NU:
+                ac_quant(n - 1)
+            if n in (0, 1):
+                lab_quant(n)
+            if n in (7, 8):
+                d2_quant(n - 7)
+            if n == NU + 1:
+                y_blocks(0, 0)
+                y_blocks(0, 1)
+            if n >= 3:
+                c_blocks((n - 3) // 2, (n - 3) % 2, n > NU)
+        y_blocks(1, 0)
+        y_blocks(1, 1)

@@ -19,6 +19,22 @@ P = 128
 FLOPS = 2 * (T * K * (F1 + F2) + T * (F1 + F2) * (N + R))
 NG = 5
 NU = 2 * NG
+SHARE = {}
+LABS = 2
+XR = 3
+ABUF = 5
+ACB = 6
+EB = 4
+ECB = 4
+MIXB = 3
+RV = 99
+WV = 99
+CV = 7
+PB = (3, 2, 3)
+YT = ['s1', 's1']
+LOADS = [('e0', 0), ('e0', 1), ('lab', 0), ('x', 0, 0, 0, 1), ('x', 0, 0, 3, 4), ('x', 0, 0, 1, 2), ('x', 0, 0, 2, 3), ('x', 0, 1, 0, 2), ('e', 1, 0), ('x', 0, 1, 2, 4), ('lab', 1), ('e', 1, 1), ('x', 1, 0, 0, 4), ('e', 3, 1), ('e', 3, 0), ('d2', 1), ('d2', 0), ('d',), ('x', 1, 1, 0, 4)]
+UNITS = [(0, 0), (0, 1), (1, 0), (1, 1), (2, 0), (2, 1), (3, 0), (4, 0), (3, 1), (4, 1)]
+PLAN = [('em', 0, 0), ('eq', 0, 0), ('em', 0, 1), ('eq', 0, 1), ('lw', 0), ('xt', 0, 0, 0), ('xq', 0, 0, 0), ('xt', 0, 0, 1), ('xq', 0, 0, 1), ('xt', 0, 0, 2), ('lm', 0), ('xq', 0, 0, 2), ('xt', 0, 0, 3), ('xq', 0, 0, 3), ('lq', 0), ('s1', 0, 0), ('em', 1, 0), ('s1', 0, 1), ('xt', 0, 1, 0), ('s1', 0, 2), ('xq', 0, 1, 0), ('xt', 0, 1, 1), ('s1', 0, 3), ('eq', 1, 0), ('xq', 0, 1, 1), ('am', 0), ('xt', 0, 1, 2), ('xq', 0, 1, 2), ('xt', 0, 1, 3), ('em', 1, 1), ('xq', 0, 1, 3), ('s1', 1, 0), ('eq', 1, 1), ('s1', 1, 1), ('tr', 0, 1), ('s1', 1, 2), ('tr', 0, 0), ('at', 0), ('em', 2, 0), ('lw', 1), ('s1', 1, 3), ('am', 1), ('ac', 0), ('eq', 2, 0), ('s1', 2, 0), ('em', 2, 1), ('lm', 1), ('s1', 2, 1), ('tr', 1, 1), ('s1', 2, 2), ('tr', 1, 0), ('at', 1), ('eq', 2, 1), ('xt', 1, 0, 0), ('s1', 2, 3), ('lq', 1), ('xq', 1, 0, 0), ('em', 3, 0), ('ac', 1), ('xt', 1, 0, 1), ('xq', 1, 0, 1), ('am', 2), ('xt', 1, 0, 2), ('s1', 3, 0), ('eq', 3, 0), ('xq', 1, 0, 2), ('s1', 3, 1), ('xt', 1, 0, 3), ('tr', 2, 1), ('em', 3, 1), ('s1', 3, 2), ('xq', 1, 0, 3), ('tr', 2, 0), ('at', 2), ('s1', 3, 3), ('eq', 3, 1), ('ac', 2), ('em', 4, 0), ('am', 3), ('s1', 4, 0), ('s1', 4, 1), ('eq', 4, 0), ('tr', 3, 1), ('s1', 4, 2), ('tr', 3, 0), ('at', 3), ('c', 0, 0), ('s1', 4, 3), ('em', 4, 1), ('c', 0, 1), ('ac', 3), ('eq', 4, 1), ('c', 0, 2), ('s1', 5, 0), ('am', 4), ('s1', 5, 1), ('c', 0, 3), ('tr', 4, 1), ('xt', 1, 1, 0), ('s1', 5, 2), ('tr', 4, 0), ('at', 4), ('xq', 1, 1, 0), ('s1', 5, 3), ('xt', 1, 1, 1), ('ac', 4), ('xq', 1, 1, 1), ('xt', 1, 1, 2), ('xq', 1, 1, 2), ('s1', 6, 0), ('xt', 1, 1, 3), ('s1', 6, 1), ('xq', 1, 1, 3), ('am', 5), ('s1', 6, 2), ('tr', 5, 1), ('tr', 5, 0), ('at', 5), ('s1', 6, 3), ('dm', 0), ('ac', 5), ('c', 1, 0), ('s1', 7, 0), ('c', 1, 1), ('dq', 0), ('dm', 1), ('s1', 7, 1), ('c', 1, 2), ('s1', 7, 2), ('tr', 6, 1), ('tr', 6, 0), ('at', 6), ('am', 6), ('s1', 7, 3), ('dq', 1), ('c', 1, 3), ('ac', 6), ('s1', 8, 0), ('s1', 8, 1), ('s1', 8, 2), ('tr', 7, 1), ('tr', 7, 0), ('at', 7), ('s1', 8, 3), ('am', 7), ('ac', 7), ('s1', 9, 0), ('s1', 9, 1), ('c', 2, 0), ('s1', 9, 2), ('tr', 8, 1), ('tr', 8, 0), ('at', 8), ('yp', 0, 0, 0, 4), ('c', 2, 1), ('s1', 9, 3), ('c', 2, 2), ('am', 8), ('ac', 8), ('yp', 0, 0, 4, 5), ('yo', 0, 0, 0), ('c', 2, 3), ('yp', 0, 1, 0, 4), ('tr', 9, 1), ('tr', 9, 0), ('at', 9), ('yp', 0, 1, 4, 5), ('yo', 0, 1, 1), ('yp', 0, 2, 0, 4), ('am', 9), ('ac', 9), ('yp', 0, 2, 4, 5), ('yo', 0, 2, 0), ('yp', 0, 3, 0, 4), ('c', 3, 0), ('yp', 0, 3, 4, 5), ('yo', 0, 3, 1), ('c', 3, 1), ('c', 3, 2), ('c', 3, 3), ('yp', 1, 0, 0, 4), ('yp', 1, 0, 4, 5), ('yo', 1, 0, 0), ('yp', 1, 1, 0, 4), ('c', 4, 0), ('yp', 1, 1, 4, 5), ('yo', 1, 1, 1), ('c', 4, 1), ('c', 4, 2), ('yp', 1, 2, 0, 4), ('c', 4, 3), ('yp', 1, 2, 4, 5), ('yo', 1, 2, 0), ('yp', 1, 3, 0, 4), ('yp', 1, 3, 4, 5), ('yo', 1, 3, 1)]
 
 
 def tile_cross_layer_transcoder_s8_kernel(
@@ -50,7 +66,7 @@ def tile_cross_layer_transcoder_s8_kernel(
         xs = [x1, x2]
 
         def load_x(s, g, parts):
-            t = tile([P, 4, K], BF16, "x_raw", 3)
+            t = tile([P, 4, K], BF16, "x_raw", XR)
             view = xs[s].rearrange("(g p j) k -> g p j k", p=P, j=4)[g]
             step = 4 // parts
             for i in range(parts):
@@ -65,48 +81,62 @@ def tile_cross_layer_transcoder_s8_kernel(
             for i in range(width // 512):
                 e_raw[g0 + i, q] = t[:, :, i * 512 : (i + 1) * 512]
 
-        t0 = tile([P, 4, K], BF16, "x_raw", 3)
-        x_raw[0, 0] = t0
-        v0 = x1.rearrange("(g p j) k -> g p j k", p=P, j=4)[0]
-        load_e(0, 0, 512, "e_a", 2, e1, 0)
-        nc.sync.dma_start(out=t0[:, 0:1, :], in_=v0[:, 0:1, :])
-        load_e(0, 1, 512, "e_a", 2, e1, 0)
-        for j in (1, 2, 3):
-            nc.sync.dma_start(out=t0[:, j : j + 1, :], in_=v0[:, j : j + 1, :])
-        load_x(0, 1, 2)
-        load_e(1, 0, 1024, "e_b", 4, e1, 512)
-        load_e(1, 1, 1024, "e_b", 4, e1, 512)
         lab_sc = keep.tile([P, 2, 4], F32, name="lab_sc", align_bytes=64)
-        nc.sync.dma_start(out=lab_sc[:], in_=labels_scale.rearrange("(g p j) o -> p g (j o)", p=P, j=4))
         lab_raw = keep.tile([P, 2, 4, R], U8, name="lab_raw", align_bytes=64)
-        nc.sync.dma_start(out=lab_raw[:], in_=labels_bytes.rearrange("(g p j) r -> p g j r", p=P, j=4))
-        load_x(1, 0, 1)
-        load_e(3, 0, 1024, "e_b", 4, e2, 0)
-        load_e(3, 1, 1024, "e_b", 4, e2, 0)
-        load_x(1, 1, 1)
         d1_w = keep.tile([P, 3, 1024], U8, name="d1_w", align_bytes=64)
-        nc.sync.dma_start(out=d1_w[:], in_=d1_words.rearrange("g p c -> p g c"))
         d1_si = d1_scales.bitcast(I32)
-        for quad in range(4):
-            nc.sync.dma_start(
-                out=d1_sc[32 * quad : 32 * quad + 4, :, :].rearrange("p g n -> p (g n)").bitcast(I32).rearrange(
-                    "p (g n) -> p g n", g=3
-                ),
-                in_=d1_si[:, 4 * quad : 4 * quad + 4, :].rearrange("g r n -> r g n"),
-            )
         d2_raw = {}
-        for g in range(2):
+        outs = {}
+
+        def ld_x(s, g, j0, j1):
+            if (s, g) not in x_raw:
+                x_raw[s, g] = tile([P, 4, K], BF16, "x_raw", XR)
+            view = xs[s].rearrange("(g p j) k -> g p j k", p=P, j=4)[g]
+            nc.sync.dma_start(out=x_raw[s, g][:, j0:j1, :], in_=view[:, j0:j1, :])
+
+        def ld_e0(q):
+            load_e(0, q, 512, "e_a", 2, e1, 0)
+
+        def ld_e(G, q):
+            if G == 1:
+                load_e(1, q, 1024, "e_b", EB, e1, 512)
+            else:
+                load_e(3, q, 1024, "e_b", EB, e2, 0)
+
+        def ld_lab(g):
+            if "sc" not in outs:
+                outs["sc"] = 1
+                nc.sync.dma_start(out=lab_sc[:], in_=labels_scale.rearrange("(g p j) o -> p g (j o)", p=P, j=4))
+            nc.sync.dma_start(
+                out=lab_raw[:, g, :, :], in_=labels_bytes.rearrange("(g p j) r -> g p j r", p=P, j=4)[g]
+            )
+
+        def ld_d():
+            nc.sync.dma_start(out=d1_w[:], in_=d1_words.rearrange("g p c -> p g c"))
+            for quad in range(4):
+                nc.sync.dma_start(
+                    out=d1_sc[32 * quad : 32 * quad + 4, :, :].rearrange("p g n -> p (g n)").bitcast(I32).rearrange(
+                        "p (g n) -> p g n", g=3
+                    ),
+                    in_=d1_si[:, 4 * quad : 4 * quad + 4, :].rearrange("g r n -> r g n"),
+                )
+
+        def ld_d2(g):
             t = tile([P, 4, N], BF16, "e_a", 2)
             nc.sync.dma_start(out=t[:], in_=d2.rearrange("(g p j) n -> g p j n", p=P, j=4)[g])
             d2_raw[g] = t
 
+        LD = dict(x=ld_x, e0=ld_e0, e=ld_e, lab=ld_lab, d=ld_d, d2=ld_d2)
+        for op in LOADS:
+            LD[op[0]](*op[1:])
+
         x_c, x_s, x_t = {}, {}, {}
 
         def x_turn(s, g, j):
-            if j == 0:
+            if (s, g) not in x_c:
                 x_c[s, g] = tile([P, 1024], U32, "x_c", 4)
                 x_s[s, g] = tile([P, 1024], U8, "x_s", 4)
-            tr = bank("tr", 2)
+            tr = bank("tr", PB[1])
             words = x_raw[s, g][:, j, :].bitcast(F32)
             for q in range(2):
                 for u in range(2):
@@ -127,9 +157,14 @@ def tile_cross_layer_transcoder_s8_kernel(
                 out=x_c[s, g][:, cols].bitcast(E4M3X4), scales=x_s[s, g][:, cols], in_=x_t[s, g, j][:]
             )
 
-        def interleave(raw):
-            t = tile([P, 512, 4], BF16, "mix", 3)
-            nc.vector.tensor_copy(out=t[:], in_=raw.rearrange("p j c -> p c j"))
+        def interleave(raw, share=0):
+            t = tile([P, 512, 4], BF16, "mix", MIXB)
+            src = raw.rearrange("p j c -> p c j")
+            cut = 512 - share
+            if share:
+                nc.scalar.copy(out=t[:, cut:, :], in_=src[:, cut:, :])
+            if cut:
+                nc.vector.tensor_copy(out=t[:, :cut, :], in_=src[:, :cut, :])
             return t
 
         def quant(codes, scales, src):
@@ -138,10 +173,10 @@ def tile_cross_layer_transcoder_s8_kernel(
         e_c, e_s, e_m = {}, {}, {}
 
         def e_mix(G, q):
-            if q == 0:
-                e_c[G] = tile([P, 2, 512], U32, "e_c", 4)
-                e_s[G] = tile([P, 2, 512], U8, "e_s", 4)
-            e_m[G, q] = interleave(e_raw[G, q])
+            if G not in e_c:
+                e_c[G] = tile([P, 2, 512], U32, "e_c", ECB)
+                e_s[G] = tile([P, 2, 512], U8, "e_s", ECB)
+            e_m[G, q] = interleave(e_raw[G, q], SHARE.get((G, q), 0))
 
         def e_quant(G, q):
             quant(e_c[G][:, q, :], e_s[G][:, q, :], e_m[G, q])
@@ -151,8 +186,16 @@ def tile_cross_layer_transcoder_s8_kernel(
         lab_b, lab_m = {}, {}
 
         def lab_widen(g):
-            t = tile([P, 4, R], BF16, "lab_b", 1)
+            t = tile([P, 4, R], BF16, "mix", MIXB)
             for j in range(4):
+                if j < LABS:
+                    nc.scalar.activation(
+                        out=t[:, j, :],
+                        in_=lab_raw[:, g, j, :].bitcast(E4M3),
+                        func=ACT.Copy,
+                        scale=lab_sc[:, g, j : j + 1],
+                    )
+                    continue
                 nc.vector.tensor_scalar(
                     out=t[:, j, :],
                     in0=lab_raw[:, g, j, :].bitcast(E4M3),
@@ -181,44 +224,44 @@ def tile_cross_layer_transcoder_s8_kernel(
         a_raw, a_m, a_t = {}, {}, {}
         ac_c, ac_s, at_c, at_s = {}, {}, {}, {}
 
-        def stage1(n):
-            G, g = divmod(n, 2)
+        def stage1(n, j):
+            G, g = UNITS[n]
             s = 0 if G < 3 else 1
-            a = tile([P, 4, 512], BF16, "a", 3)
-            a_raw[n] = a
-            for j in range(4):
-                acc = bank("s1", 3)
-                for q in range(2):
-                    cols = slice(256 * j + 128 * q, 256 * j + 128 * (q + 1))
-                    nc.tensor.matmul_mx(
-                        out=acc[:],
-                        lhsT=x_c[s, g][:, cols].bitcast(E4M3X4),
-                        lhsT_scale=x_s[s, g][:, cols],
-                        rhs=e_c[G][:, q, :].bitcast(E4M3X4),
-                        rhs_scale=e_s[G][:, q, :],
-                        start=(q == 0),
-                        stop=(q == 1),
-                    )
-                nc.scalar.activation(
-                    out=a[:, j, :].rearrange("p (u m e) -> p u m e", u=2, e=2),
-                    in_=acc[:].rearrange("p (m u e) -> p u m e", u=2, e=2),
-                    func=ACT.Relu,
+            if n not in a_raw:
+                a_raw[n] = tile([P, 4, 512], BF16, "a", ABUF)
+            a = a_raw[n]
+            acc = bank("s1", PB[0])
+            for q in range(2):
+                cols = slice(256 * j + 128 * q, 256 * j + 128 * (q + 1))
+                nc.tensor.matmul_mx(
+                    out=acc[:],
+                    lhsT=x_c[s, g][:, cols].bitcast(E4M3X4),
+                    lhsT_scale=x_s[s, g][:, cols],
+                    rhs=e_c[G][:, q, :].bitcast(E4M3X4),
+                    rhs_scale=e_s[G][:, q, :],
+                    start=(q == 0),
+                    stop=(q == 1),
                 )
+            out = a[:, j, :].rearrange("p (u m e) -> p u m e", u=2, e=2)
+            src = acc[:].rearrange("p (m u e) -> p u m e", u=2, e=2)
+            if n >= RV and j == 3:
+                nc.vector.tensor_scalar_max(out, src, 0.0)
+            else:
+                nc.scalar.activation(out=out, in_=src, func=ACT.Relu)
 
-        def a_turn(n):
-            at = tile([P, 512, 4], BF16, "a_t", 2)
-            a_t[n] = at
+        def a_turn(n, h):
+            if n not in a_t:
+                a_t[n] = tile([P, 512, 4], BF16, "a_t", 2)
             words = a_raw[n][:].rearrange("p j f -> p (j f)").bitcast(F32)
-            out = at[:].rearrange("p t f -> p (t f)").bitcast(F32)
-            for h in range(2):
-                tr = bank("tr", 2)
-                for i in range(4):
-                    col = 512 * h + 128 * i
-                    nc.tensor.transpose(tr[:, i * P : (i + 1) * P], words[:, col : col + P], ident[:])
-                nc.scalar.copy(
-                    out=out[:, 512 * h : 512 * (h + 1)].rearrange("p (j t u) -> p j t u", j=2, u=2),
-                    in_=tr[:].rearrange("p (j u t) -> p j t u", j=2, u=2),
-                )
+            out = a_t[n][:].rearrange("p t f -> p (t f)").bitcast(F32)
+            tr = bank("tr", PB[1])
+            for i in range(4):
+                col = 512 * h + 128 * i
+                nc.tensor.transpose(tr[:, i * P : (i + 1) * P], words[:, col : col + P], ident[:])
+            (nc.vector.tensor_copy if (n >= WV and h == 1) else nc.scalar.copy)(
+                out=out[:, 512 * h : 512 * (h + 1)].rearrange("p (j t u) -> p j t u", j=2, u=2),
+                in_=tr[:].rearrange("p (j u t) -> p j t u", j=2, u=2),
+            )
 
         def a_mix(n):
             t = tile([P, 512, 4], BF16, "a_m", 2)
@@ -229,8 +272,8 @@ def tile_cross_layer_transcoder_s8_kernel(
             a_m[n] = t
 
         def ac_quant(n):
-            ac_c[n] = tile([P, 512], U32, "ac_c", 6)
-            ac_s[n] = tile([P, 512], U8, "ac_s", 6)
+            ac_c[n] = tile([P, 512], U32, "ac_c", ACB)
+            ac_s[n] = tile([P, 512], U8, "ac_s", ACB)
             quant(ac_c[n][:], ac_s[n][:], a_m[n])
 
         def at_quant(n):
@@ -238,109 +281,69 @@ def tile_cross_layer_transcoder_s8_kernel(
             at_s[n] = tile([P, 512], U8, "at_s", NU)
             quant(at_c[n][:], at_s[n][:], a_t[n])
 
-        outs = {}
+        def c_block(G, b):
+            half, i = divmod(b, 2)
+            if i == 0:
+                outs["c", G, half] = tile([P, 2, R], F32, "o", 4)
+            o = outs["c", G, half]
+            acc = bank("o", PB[2])
+            cols = slice(128 * b, 128 * (b + 1))
+            for g in range(2):
+                n = UNITS.index((G, g))
+                nc.tensor.matmul_mx(
+                    out=acc[:],
+                    lhsT=ac_c[n][:, cols].bitcast(E4M3X4),
+                    lhsT_scale=ac_s[n][:, cols],
+                    rhs=lab_c[:, g, :].bitcast(E4M3X4),
+                    rhs_scale=lab_s[:, g, :],
+                    start=(g == 0),
+                    stop=(g == 1),
+                )
+            if i == 1 and UNITS.index((G, 1)) >= CV:
+                nc.vector.tensor_copy(out=o[:, i, :], in_=acc[:])
+            else:
+                nc.scalar.copy(out=o[:, i, :], in_=acc[:])
+            if i == 1:
+                dst = out_1 if G < 3 else out_2
+                row = 512 * (G if G < 3 else G - 3) + 256 * half
+                nc.sync.dma_start(out=dst[row : row + 256, :].rearrange("(b p) r -> p b r", p=P), in_=o[:])
 
-        def c_blocks(G, half, vec=False):
-            o = tile([P, 2, R], F32, "o", 4)
-            for i in range(2):
-                b = 2 * half + i
-                acc = bank("o", 3)
-                cols = slice(128 * b, 128 * (b + 1))
-                for g in range(2):
-                    n = 2 * G + g
-                    nc.tensor.matmul_mx(
-                        out=acc[:],
-                        lhsT=ac_c[n][:, cols].bitcast(E4M3X4),
-                        lhsT_scale=ac_s[n][:, cols],
-                        rhs=lab_c[:, g, :].bitcast(E4M3X4),
-                        rhs_scale=lab_s[:, g, :],
-                        start=(g == 0),
-                        stop=(g == 1),
-                    )
-                if vec and i == 1:
-                    nc.vector.tensor_copy(out=o[:, i, :], in_=acc[:])
+        y_acc = {}
+
+        def y_pass(g, j, G0, G1):
+            if G0 == 0:
+                y_acc[g, j] = bank(YT[g], PB[0] if YT[g] == "s1" else PB[2])
+            cols = slice(128 * j, 128 * (j + 1))
+            for G in range(G0, G1):
+                n = UNITS.index((G, g))
+                if G < 3:
+                    rhs, rhs_scale = d1_w[:, G, :].bitcast(E2M1X4), d1_sc[:, G, :]
                 else:
-                    nc.scalar.copy(out=o[:, i, :], in_=acc[:])
-            dst = out_1 if G < 3 else out_2
-            row = 512 * (G if G < 3 else G - 3) + 256 * half
-            nc.sync.dma_start(out=dst[row : row + 256, :].rearrange("(b p) r -> p b r", p=P), in_=o[:])
+                    rhs, rhs_scale = d2_c[:, G - 3, :].bitcast(E4M3X4), d2_s[:, G - 3, :]
+                nc.tensor.matmul_mx(
+                    out=y_acc[g, j][:],
+                    lhsT=at_c[n][:, cols].bitcast(E4M3X4),
+                    lhsT_scale=at_s[n][:, cols],
+                    rhs=rhs,
+                    rhs_scale=rhs_scale,
+                    start=(G == 0),
+                    stop=(G == NG - 1),
+                )
 
-        def y_blocks(g, half):
-            o = tile([P, 2, N], F32, "o", 4)
-            for i in range(2):
-                j = 2 * half + i
-                acc = bank("o", 3)
-                cols = slice(128 * j, 128 * (j + 1))
-                for G in range(NG):
-                    n = 2 * G + g
-                    if G < 3:
-                        rhs, rhs_scale = d1_w[:, G, :].bitcast(E2M1X4), d1_sc[:, G, :]
-                    else:
-                        rhs, rhs_scale = d2_c[:, G - 3, :].bitcast(E4M3X4), d2_s[:, G - 3, :]
-                    nc.tensor.matmul_mx(
-                        out=acc[:],
-                        lhsT=at_c[n][:, cols].bitcast(E4M3X4),
-                        lhsT_scale=at_s[n][:, cols],
-                        rhs=rhs,
-                        rhs_scale=rhs_scale,
-                        start=(G == 0),
-                        stop=(G == NG - 1),
-                    )
-                if i == 1:
-                    nc.vector.tensor_copy(out=o[:, i, :], in_=acc[:])
-                else:
-                    nc.scalar.copy(out=o[:, i, :], in_=acc[:])
-            dst = out_0.rearrange("(g p j) n -> g p j n", p=P, j=4)[g]
-            nc.sync.dma_start(out=dst[:, 2 * half : 2 * half + 2, :], in_=o[:])
+        def y_out(g, j, vec):
+            if j % 2 == 0:
+                outs[g] = tile([P, 2, N], F32, "o", 4)
+            o = outs[g]
+            (nc.vector.tensor_copy if vec else nc.scalar.copy)(out=o[:, j % 2, :], in_=y_acc[g, j][:])
+            if j % 2 == 1:
+                dst = out_0.rearrange("(g p j) n -> g p j n", p=P, j=4)[g]
+                nc.sync.dma_start(out=dst[:, j - 1 : j + 1, :], in_=o[:])
 
-        for j in range(4):
-            x_turn(0, 0, j)
-        e_mix(0, 0)
-        e_mix(0, 1)
-        e_quant(0, 0)
-        x_quant(0, 0, 0)
-        e_quant(0, 1)
-        for j in range(1, 4):
-            x_quant(0, 0, j)
+        def do(op):
+            k, a = op[0], op[1:]
+            FN[k](*a)
 
-        extra_x = {0: [(0, 1, 0), (0, 1, 1), (0, 1, 2), (0, 1, 3)]}
-        for i in range(4):
-            extra_x[1 + i] = [(1, i // 2, 2 * (i % 2)), (1, i // 2, 2 * (i % 2) + 1)]
-        for n in range(NU + 3):
-            if n < NU:
-                stage1(n)
-            for s, g, j in extra_x.get(n, []):
-                x_turn(s, g, j)
-            for s, g, j in extra_x.get(n, []):
-                x_quant(s, g, j)
-            if 1 <= n <= NU:
-                a_turn(n - 1)
-                a_mix(n - 1)
-            G, q = n // 2 + 1, n % 2
-            if G < NG:
-                e_mix(G, q)
-            if n == 0:
-                lab_widen(0)
-            if n == 1:
-                lab_widen(1)
-            if 2 <= n <= NU + 1:
-                at_quant(n - 2)
-            if G < NG:
-                e_quant(G, q)
-            if n in (0, 1):
-                lab_mix(n)
-            if n in (7, 8):
-                d2_mix(n - 7)
-            if 1 <= n <= NU:
-                ac_quant(n - 1)
-            if n in (0, 1):
-                lab_quant(n)
-            if n in (7, 8):
-                d2_quant(n - 7)
-            if n == NU + 1:
-                y_blocks(0, 0)
-                y_blocks(0, 1)
-            if n >= 3:
-                c_blocks((n - 3) // 2, (n - 3) % 2, n > NU)
-        y_blocks(1, 0)
-        y_blocks(1, 1)
+        FN = dict(xt=x_turn, xq=x_quant, em=e_mix, eq=e_quant, lw=lab_widen, lm=lab_mix, lq=lab_quant, dm=d2_mix, dq=d2_quant,
+                  s1=stage1, tr=a_turn, am=a_mix, ac=ac_quant, at=at_quant, c=c_block, yp=y_pass, yo=y_out)
+        for op in PLAN:
+            do(op)

from contextlib import ExitStack

import concourse.mybir as mybir
from concourse.masks import make_identity

F32 = mybir.dt.float32
BF16 = mybir.dt.bfloat16
U32 = mybir.dt.uint32
I32 = mybir.dt.int32
U8 = mybir.dt.uint8
E4M3 = mybir.dt.float8_e4m3fn
E4M3X4 = mybir.dt.float8_e4m3fn_x4
E2M1X4 = mybir.dt.float4_e2m1fn_x4
ACT = mybir.ActivationFunctionType
ALU = mybir.AluOpType

T, K, F1, F2, N, R = 1024, 1024, 1536, 1024, 512, 512
P = 128
FLOPS = 2 * (T * K * (F1 + F2) + T * (F1 + F2) * (N + R))
NG = 5
NU = 2 * NG
SHARE = {}
LABS = 2
XR = 3
ABUF = 5
ACB = 6
EB = 4
ECB = 4
MIXB = 3
RV = 99
WV = 99
CV = 7
PB = (3, 2, 3)
YT = ['s1', 's1']
LOADS = [('e0', 0), ('e0', 1), ('lab', 0), ('x', 0, 0, 0, 1), ('x', 0, 0, 3, 4), ('x', 0, 0, 1, 2), ('x', 0, 0, 2, 3), ('x', 0, 1, 0, 2), ('e', 1, 0), ('x', 0, 1, 2, 4), ('lab', 1), ('e', 1, 1), ('x', 1, 0, 0, 4), ('e', 3, 1), ('e', 3, 0), ('d2', 1), ('d2', 0), ('d',), ('x', 1, 1, 0, 4)]
UNITS = [(0, 0), (0, 1), (1, 0), (1, 1), (2, 0), (2, 1), (3, 0), (4, 0), (3, 1), (4, 1)]
PLAN = [('em', 0, 0), ('eq', 0, 0), ('em', 0, 1), ('eq', 0, 1), ('lw', 0), ('xt', 0, 0, 0), ('xq', 0, 0, 0), ('xt', 0, 0, 1), ('xq', 0, 0, 1), ('xt', 0, 0, 2), ('lm', 0), ('xq', 0, 0, 2), ('xt', 0, 0, 3), ('xq', 0, 0, 3), ('lq', 0), ('s1', 0, 0), ('em', 1, 0), ('s1', 0, 1), ('xt', 0, 1, 0), ('s1', 0, 2), ('xq', 0, 1, 0), ('xt', 0, 1, 1), ('s1', 0, 3), ('eq', 1, 0), ('xq', 0, 1, 1), ('am', 0), ('xt', 0, 1, 2), ('xq', 0, 1, 2), ('xt', 0, 1, 3), ('em', 1, 1), ('xq', 0, 1, 3), ('s1', 1, 0), ('eq', 1, 1), ('s1', 1, 1), ('tr', 0, 1), ('s1', 1, 2), ('tr', 0, 0), ('at', 0), ('em', 2, 0), ('lw', 1), ('s1', 1, 3), ('am', 1), ('ac', 0), ('eq', 2, 0), ('s1', 2, 0), ('em', 2, 1), ('lm', 1), ('s1', 2, 1), ('tr', 1, 1), ('s1', 2, 2), ('tr', 1, 0), ('at', 1), ('eq', 2, 1), ('xt', 1, 0, 0), ('s1', 2, 3), ('lq', 1), ('xq', 1, 0, 0), ('em', 3, 0), ('ac', 1), ('xt', 1, 0, 1), ('xq', 1, 0, 1), ('am', 2), ('xt', 1, 0, 2), ('s1', 3, 0), ('eq', 3, 0), ('xq', 1, 0, 2), ('s1', 3, 1), ('xt', 1, 0, 3), ('tr', 2, 1), ('em', 3, 1), ('s1', 3, 2), ('xq', 1, 0, 3), ('tr', 2, 0), ('at', 2), ('s1', 3, 3), ('eq', 3, 1), ('ac', 2), ('em', 4, 0), ('am', 3), ('s1', 4, 0), ('s1', 4, 1), ('eq', 4, 0), ('tr', 3, 1), ('s1', 4, 2), ('tr', 3, 0), ('at', 3), ('c', 0, 0), ('s1', 4, 3), ('em', 4, 1), ('c', 0, 1), ('ac', 3), ('eq', 4, 1), ('c', 0, 2), ('s1', 5, 0), ('am', 4), ('s1', 5, 1), ('c', 0, 3), ('tr', 4, 1), ('xt', 1, 1, 0), ('s1', 5, 2), ('tr', 4, 0), ('at', 4), ('xq', 1, 1, 0), ('s1', 5, 3), ('xt', 1, 1, 1), ('ac', 4), ('xq', 1, 1, 1), ('xt', 1, 1, 2), ('xq', 1, 1, 2), ('s1', 6, 0), ('xt', 1, 1, 3), ('s1', 6, 1), ('xq', 1, 1, 3), ('am', 5), ('s1', 6, 2), ('tr', 5, 1), ('tr', 5, 0), ('at', 5), ('s1', 6, 3), ('dm', 0), ('ac', 5), ('c', 1, 0), ('s1', 7, 0), ('c', 1, 1), ('dq', 0), ('dm', 1), ('s1', 7, 1), ('c', 1, 2), ('s1', 7, 2), ('tr', 6, 1), ('tr', 6, 0), ('at', 6), ('am', 6), ('s1', 7, 3), ('dq', 1), ('c', 1, 3), ('ac', 6), ('s1', 8, 0), ('s1', 8, 1), ('s1', 8, 2), ('tr', 7, 1), ('tr', 7, 0), ('at', 7), ('s1', 8, 3), ('am', 7), ('ac', 7), ('s1', 9, 0), ('s1', 9, 1), ('c', 2, 0), ('s1', 9, 2), ('tr', 8, 1), ('tr', 8, 0), ('at', 8), ('yp', 0, 0, 0, 4), ('c', 2, 1), ('s1', 9, 3), ('c', 2, 2), ('am', 8), ('ac', 8), ('yp', 0, 0, 4, 5), ('yo', 0, 0, 0), ('c', 2, 3), ('yp', 0, 1, 0, 4), ('tr', 9, 1), ('tr', 9, 0), ('at', 9), ('yp', 0, 1, 4, 5), ('yo', 0, 1, 1), ('yp', 0, 2, 0, 4), ('am', 9), ('ac', 9), ('yp', 0, 2, 4, 5), ('yo', 0, 2, 0), ('yp', 0, 3, 0, 4), ('c', 3, 0), ('yp', 0, 3, 4, 5), ('yo', 0, 3, 1), ('c', 3, 1), ('c', 3, 2), ('c', 3, 3), ('yp', 1, 0, 0, 4), ('yp', 1, 0, 4, 5), ('yo', 1, 0, 0), ('yp', 1, 1, 0, 4), ('c', 4, 0), ('yp', 1, 1, 4, 5), ('yo', 1, 1, 1), ('c', 4, 1), ('c', 4, 2), ('yp', 1, 2, 0, 4), ('c', 4, 3), ('yp', 1, 2, 4, 5), ('yo', 1, 2, 0), ('yp', 1, 3, 0, 4), ('yp', 1, 3, 4, 5), ('yo', 1, 3, 1)]


def tile_cross_layer_transcoder_s8_kernel(
    tc, x1, x2, e1, e2, d1_words, d1_scales, d2, labels_bytes, labels_scale, out_0, out_1, out_2
):
    nc = tc.nc
    with ExitStack() as ctx:
        keep = ctx.enter_context(tc.tile_pool(name="keep", bufs=1))
        pool = ctx.enter_context(tc.tile_pool(name="work", bufs=1))
        psum = ctx.enter_context(tc.psum_pool(name="psum", bufs=1))
        ctx.enter_context(tc.manual_schedule())

        def tile(shape, dtype, tag, bufs):
            return pool.tile(shape, dtype, name=tag, tag=tag, bufs=bufs, align_bytes=64)

        def bank(tag, bufs):
            return psum.tile([P, 512], F32, name=tag, tag=tag, bufs=bufs)

        ident = keep.tile([P, P], F32, name="ident", align_bytes=64)
        make_identity(nc, ident[:])
        warm = keep.tile([P, 1], F32, name="warm", align_bytes=64)
        nc.gpsimd.memset(warm[:], 0.0)
        nc.scalar.activation(out=warm[:], in_=warm[:], func=ACT.Relu)
        d1_sc = keep.tile([P, 3, 512], U8, name="d1_sc", align_bytes=64)
        nc.gpsimd.memset(d1_sc[:].rearrange("p g n -> p (g n)").bitcast(I32), 0)

        x_raw = {}
        e_raw = {}
        xs = [x1, x2]

        def load_x(s, g, parts):
            t = tile([P, 4, K], BF16, "x_raw", XR)
            view = xs[s].rearrange("(g p j) k -> g p j k", p=P, j=4)[g]
            step = 4 // parts
            for i in range(parts):
                nc.sync.dma_start(out=t[:, i * step : (i + 1) * step, :], in_=view[:, i * step : (i + 1) * step, :])
            x_raw[s, g] = t

        def load_e(g0, q, width, tag, bufs, e, col):
            t = tile([P, 4, width], BF16, tag, bufs)
            nc.sync.dma_start(
                out=t[:], in_=e.rearrange("(q p j) c -> q p j c", p=P, j=4)[q][:, :, col : col + width]
            )
            for i in range(width // 512):
                e_raw[g0 + i, q] = t[:, :, i * 512 : (i + 1) * 512]

        lab_sc = keep.tile([P, 2, 4], F32, name="lab_sc", align_bytes=64)
        lab_raw = keep.tile([P, 2, 4, R], U8, name="lab_raw", align_bytes=64)
        d1_w = keep.tile([P, 3, 1024], U8, name="d1_w", align_bytes=64)
        d1_si = d1_scales.bitcast(I32)
        d2_raw = {}
        outs = {}

        def ld_x(s, g, j0, j1):
            if (s, g) not in x_raw:
                x_raw[s, g] = tile([P, 4, K], BF16, "x_raw", XR)
            view = xs[s].rearrange("(g p j) k -> g p j k", p=P, j=4)[g]
            nc.sync.dma_start(out=x_raw[s, g][:, j0:j1, :], in_=view[:, j0:j1, :])

        def ld_e0(q):
            load_e(0, q, 512, "e_a", 2, e1, 0)

        def ld_e(G, q):
            if G == 1:
                load_e(1, q, 1024, "e_b", EB, e1, 512)
            else:
                load_e(3, q, 1024, "e_b", EB, e2, 0)

        def ld_lab(g):
            if "sc" not in outs:
                outs["sc"] = 1
                nc.sync.dma_start(out=lab_sc[:], in_=labels_scale.rearrange("(g p j) o -> p g (j o)", p=P, j=4))
            nc.sync.dma_start(
                out=lab_raw[:, g, :, :], in_=labels_bytes.rearrange("(g p j) r -> g p j r", p=P, j=4)[g]
            )

        def ld_d():
            nc.sync.dma_start(out=d1_w[:], in_=d1_words.rearrange("g p c -> p g c"))
            for quad in range(4):
                nc.sync.dma_start(
                    out=d1_sc[32 * quad : 32 * quad + 4, :, :].rearrange("p g n -> p (g n)").bitcast(I32).rearrange(
                        "p (g n) -> p g n", g=3
                    ),
                    in_=d1_si[:, 4 * quad : 4 * quad + 4, :].rearrange("g r n -> r g n"),
                )

        def ld_d2(g):
            t = tile([P, 4, N], BF16, "e_a", 2)
            nc.sync.dma_start(out=t[:], in_=d2.rearrange("(g p j) n -> g p j n", p=P, j=4)[g])
            d2_raw[g] = t

        LD = dict(x=ld_x, e0=ld_e0, e=ld_e, lab=ld_lab, d=ld_d, d2=ld_d2)
        for op in LOADS:
            LD[op[0]](*op[1:])

        x_c, x_s, x_t = {}, {}, {}

        def x_turn(s, g, j):
            if (s, g) not in x_c:
                x_c[s, g] = tile([P, 1024], U32, "x_c", 4)
                x_s[s, g] = tile([P, 1024], U8, "x_s", 4)
            tr = bank("tr", PB[1])
            words = x_raw[s, g][:, j, :].bitcast(F32)
            for q in range(2):
                for u in range(2):
                    i = 2 * q + u
                    nc.tensor.transpose(
                        tr[:, i * P : (i + 1) * P], words[:, 256 * q + u : 256 * (q + 1) : 2], ident[:]
                    )
            xt = tile([P, 1024], BF16, "x_t", 4)
            nc.scalar.copy(
                out=xt[:].bitcast(F32).rearrange("p (q t u) -> p q t u", q=2, u=2),
                in_=tr[:].rearrange("p (q u t) -> p q t u", q=2, u=2),
            )
            x_t[s, g, j] = xt

        def x_quant(s, g, j):
            cols = slice(256 * j, 256 * (j + 1))
            nc.vector.quantize_mx(
                out=x_c[s, g][:, cols].bitcast(E4M3X4), scales=x_s[s, g][:, cols], in_=x_t[s, g, j][:]
            )

        def interleave(raw, share=0):
            t = tile([P, 512, 4], BF16, "mix", MIXB)
            src = raw.rearrange("p j c -> p c j")
            cut = 512 - share
            if share:
                nc.scalar.copy(out=t[:, cut:, :], in_=src[:, cut:, :])
            if cut:
                nc.vector.tensor_copy(out=t[:, :cut, :], in_=src[:, :cut, :])
            return t

        def quant(codes, scales, src):
            nc.vector.quantize_mx(out=codes.bitcast(E4M3X4), scales=scales, in_=src[:].rearrange("p c j -> p (c j)"))

        e_c, e_s, e_m = {}, {}, {}

        def e_mix(G, q):
            if G not in e_c:
                e_c[G] = tile([P, 2, 512], U32, "e_c", ECB)
                e_s[G] = tile([P, 2, 512], U8, "e_s", ECB)
            e_m[G, q] = interleave(e_raw[G, q], SHARE.get((G, q), 0))

        def e_quant(G, q):
            quant(e_c[G][:, q, :], e_s[G][:, q, :], e_m[G, q])

        lab_c = keep.tile([P, 2, R], U32, name="lab_c", align_bytes=64)
        lab_s = keep.tile([P, 2, R], U8, name="lab_s", align_bytes=64)
        lab_b, lab_m = {}, {}

        def lab_widen(g):
            t = tile([P, 4, R], BF16, "mix", MIXB)
            for j in range(4):
                if j < LABS:
                    nc.scalar.activation(
                        out=t[:, j, :],
                        in_=lab_raw[:, g, j, :].bitcast(E4M3),
                        func=ACT.Copy,
                        scale=lab_sc[:, g, j : j + 1],
                    )
                    continue
                nc.vector.tensor_scalar(
                    out=t[:, j, :],
                    in0=lab_raw[:, g, j, :].bitcast(E4M3),
                    scalar1=lab_sc[:, g, j : j + 1],
                    scalar2=None,
                    op0=ALU.mult,
                )
            lab_b[g] = t

        def lab_mix(g):
            lab_m[g] = interleave(lab_b[g][:])

        def lab_quant(g):
            quant(lab_c[:, g, :], lab_s[:, g, :], lab_m[g])

        d2_c = keep.tile([P, 2, N], U32, name="d2_c", align_bytes=64)
        d2_s = keep.tile([P, 2, N], U8, name="d2_s", align_bytes=64)
        d2_m = {}

        def d2_mix(g):
            d2_m[g] = interleave(d2_raw[g][:])

        def d2_quant(g):
            quant(d2_c[:, g, :], d2_s[:, g, :], d2_m[g])

        a_raw, a_m, a_t = {}, {}, {}
        ac_c, ac_s, at_c, at_s = {}, {}, {}, {}

        def stage1(n, j):
            G, g = UNITS[n]
            s = 0 if G < 3 else 1
            if n not in a_raw:
                a_raw[n] = tile([P, 4, 512], BF16, "a", ABUF)
            a = a_raw[n]
            acc = bank("s1", PB[0])
            for q in range(2):
                cols = slice(256 * j + 128 * q, 256 * j + 128 * (q + 1))
                nc.tensor.matmul_mx(
                    out=acc[:],
                    lhsT=x_c[s, g][:, cols].bitcast(E4M3X4),
                    lhsT_scale=x_s[s, g][:, cols],
                    rhs=e_c[G][:, q, :].bitcast(E4M3X4),
                    rhs_scale=e_s[G][:, q, :],
                    start=(q == 0),
                    stop=(q == 1),
                )
            out = a[:, j, :].rearrange("p (u m e) -> p u m e", u=2, e=2)
            src = acc[:].rearrange("p (m u e) -> p u m e", u=2, e=2)
            if n >= RV and j == 3:
                nc.vector.tensor_scalar_max(out, src, 0.0)
            else:
                nc.scalar.activation(out=out, in_=src, func=ACT.Relu)

        def a_turn(n, h):
            if n not in a_t:
                a_t[n] = tile([P, 512, 4], BF16, "a_t", 2)
            words = a_raw[n][:].rearrange("p j f -> p (j f)").bitcast(F32)
            out = a_t[n][:].rearrange("p t f -> p (t f)").bitcast(F32)
            tr = bank("tr", PB[1])
            for i in range(4):
                col = 512 * h + 128 * i
                nc.tensor.transpose(tr[:, i * P : (i + 1) * P], words[:, col : col + P], ident[:])
            (nc.vector.tensor_copy if (n >= WV and h == 1) else nc.scalar.copy)(
                out=out[:, 512 * h : 512 * (h + 1)].rearrange("p (j t u) -> p j t u", j=2, u=2),
                in_=tr[:].rearrange("p (j u t) -> p j t u", j=2, u=2),
            )

        def a_mix(n):
            t = tile([P, 512, 4], BF16, "a_m", 2)
            src = a_raw[n][:].rearrange("p j (u m e) -> p u m e j", u=2, e=2)
            dst = t[:].rearrange("p (m u e) j -> p u m e j", u=2, e=2)
            for u in range(2):
                nc.vector.tensor_copy(out=dst[:, u], in_=src[:, u])
            a_m[n] = t

        def ac_quant(n):
            ac_c[n] = tile([P, 512], U32, "ac_c", ACB)
            ac_s[n] = tile([P, 512], U8, "ac_s", ACB)
            quant(ac_c[n][:], ac_s[n][:], a_m[n])

        def at_quant(n):
            at_c[n] = tile([P, 512], U32, "at_c", NU)
            at_s[n] = tile([P, 512], U8, "at_s", NU)
            quant(at_c[n][:], at_s[n][:], a_t[n])

        def c_block(G, b):
            half, i = divmod(b, 2)
            if i == 0:
                outs["c", G, half] = tile([P, 2, R], F32, "o", 4)
            o = outs["c", G, half]
            acc = bank("o", PB[2])
            cols = slice(128 * b, 128 * (b + 1))
            for g in range(2):
                n = UNITS.index((G, g))
                nc.tensor.matmul_mx(
                    out=acc[:],
                    lhsT=ac_c[n][:, cols].bitcast(E4M3X4),
                    lhsT_scale=ac_s[n][:, cols],
                    rhs=lab_c[:, g, :].bitcast(E4M3X4),
                    rhs_scale=lab_s[:, g, :],
                    start=(g == 0),
                    stop=(g == 1),
                )
            if i == 1 and UNITS.index((G, 1)) >= CV:
                nc.vector.tensor_copy(out=o[:, i, :], in_=acc[:])
            else:
                nc.scalar.copy(out=o[:, i, :], in_=acc[:])
            if i == 1:
                dst = out_1 if G < 3 else out_2
                row = 512 * (G if G < 3 else G - 3) + 256 * half
                nc.sync.dma_start(out=dst[row : row + 256, :].rearrange("(b p) r -> p b r", p=P), in_=o[:])

        y_acc = {}

        def y_pass(g, j, G0, G1):
            if G0 == 0:
                y_acc[g, j] = bank(YT[g], PB[0] if YT[g] == "s1" else PB[2])
            cols = slice(128 * j, 128 * (j + 1))
            for G in range(G0, G1):
                n = UNITS.index((G, g))
                if G < 3:
                    rhs, rhs_scale = d1_w[:, G, :].bitcast(E2M1X4), d1_sc[:, G, :]
                else:
                    rhs, rhs_scale = d2_c[:, G - 3, :].bitcast(E4M3X4), d2_s[:, G - 3, :]
                nc.tensor.matmul_mx(
                    out=y_acc[g, j][:],
                    lhsT=at_c[n][:, cols].bitcast(E4M3X4),
                    lhsT_scale=at_s[n][:, cols],
                    rhs=rhs,
                    rhs_scale=rhs_scale,
                    start=(G == 0),
                    stop=(G == NG - 1),
                )

        def y_out(g, j, vec):
            if j % 2 == 0:
                outs[g] = tile([P, 2, N], F32, "o", 4)
            o = outs[g]
            (nc.vector.tensor_copy if vec else nc.scalar.copy)(out=o[:, j % 2, :], in_=y_acc[g, j][:])
            if j % 2 == 1:
                dst = out_0.rearrange("(g p j) n -> g p j n", p=P, j=4)[g]
                nc.sync.dma_start(out=dst[:, j - 1 : j + 1, :], in_=o[:])

        def do(op):
            k, a = op[0], op[1:]
            FN[k](*a)

        FN = dict(xt=x_turn, xq=x_quant, em=e_mix, eq=e_quant, lw=lab_widen, lm=lab_mix, lq=lab_quant, dm=d2_mix, dq=d2_quant,
                  s1=stage1, tr=a_turn, am=a_mix, ac=ac_quant, at=at_quant, c=c_block, yp=y_pass, yo=y_out)
        for op in PLAN:
            do(op)
